import numpy as np, ml_dtypes
CORES = [0,1,2,3,4,5,6,7,8,9,10,11,12,13,14,15,128,129,130,131,132,133,134,135,136,137,138,139,140,141,142,143]
N = 32
GROUPS = [[0,16],[1,17],[2,18],[3,19],[4,20],[5,21],[6,22],[7,23],[8,24],[9,25],[10,26],[11,27],[12,28],[13,29],[14,30],[15,31]]
def setup_inputs(rng):
    return {"x": rng.standard_normal((N, 128, 64), dtype=np.float32).astype(ml_dtypes.bfloat16)}
def reference(x):
    y = np.empty((N, 128, 32), x.dtype)
    for g in GROUPS:
        s = x[g].sum(axis=0, dtype=np.float64).astype(x[g].dtype)
        n = len(g); b = x.shape[2] // n
        for i, r in enumerate(g):
            y[r] = s[:, i * b:(i + 1) * b]
    return {"y": y}

from concourse.mybir import AluOpType

SCRATCH = {
    "send": ("dram", [128, 32], "bfloat16"),
    "land": ("dram", [128, 32], "bfloat16"),
}
SEMAPHORES = ["loaded", "copied", "sent", "arrived", "stored"]


def rank_program(g, core, T, topo):
    rank = T.rank_of(core)
    if rank is None:
        return
    group = [grp for grp in T.tables["GROUPS"] if rank in grp][0]
    me = group.index(rank)
    peer_i = 1 - me
    peer = T.cores[group[peer_i]]
    b = T.x.shape[1] // len(group)

    g.sync.dma_start(T.send[:], T.x[:, peer_i * b:(peer_i + 1) * b]).then_inc(T.sem.loaded, 16)
    g.sync.dma_start(T.y[:], T.x[:, me * b:(me + 1) * b]).then_inc(T.sem.copied, 16)

    rid, pid = topo.addr(peer, core)
    g.wait_ge(T.sem.loaded, 16)
    g.remote_dma(T.land[:], T.send[:], T.sem.arrived, T.sem.sent, pid, rid, 0xFF)

    g.wait_ge(T.sem.copied, 16)
    g.wait_ge(T.sem.arrived, 8)
    g.dma_start(T.y[:], T.land[:], accum_op=AluOpType.add).then_inc(T.sem.stored, 16)
    g.wait_ge(T.sem.sent, 8)
    g.wait_ge(T.sem.stored, 16)
